import numpy as np, ml_dtypes
CORES = [2,10,18,26,34,42,50,58,66,74,82,90,98,106,114,122,130,138,146,154,162,170,178,186,194,202,210,218,226,234,242,250]
N = 32
H = 2
PERIODIC = True
def setup_inputs(rng):
    return {"x": rng.standard_normal((N, 128, 128), dtype=np.float32).astype(ml_dtypes.bfloat16)}
def reference(x):
    W = x.shape[2]
    y = np.zeros((N, 128, W + 2 * H), x.dtype)
    for r in range(N):
        y[r][:, H:H + W] = x[r]
        left, right = r - 1, r + 1
        if PERIODIC:
            left, right = left % N, right % N
        if 0 <= left < N:
            y[r][:, :H] = x[left][:, W - H:]
        if 0 <= right < N:
            y[r][:, W + H:] = x[right][:, :H]
    return {"y": y}

@@ -1,0 +1,45 @@
+from concourse.bass import DstId, RemoteDMATransfer
+
+H = 2
+
+SCRATCH = {
+    "send": ("dram", [2, 128, H], "bfloat16"),
+    "land": ("dram", [2, 128, H], "bfloat16"),
+}
+SEMAPHORES = ["loaded", "sent", "arr_l", "arr_r", "stored"]
+
+
+def rank_program(g, core, T, topo):
+    rank = T.rank_of(core)
+    if rank is None:
+        return
+    n = len(T.cores)
+    right = T.cores[(rank + 1) % n]
+    left = T.cores[(rank - 1) % n]
+    W = T.x.shape[1]
+    s = T.sem
+
+    g.sync.dma_start(T.send[0], T.x[:, W - H:W]).then_inc(s.loaded, 16)
+    g.scalar.dma_start(T.send[1], T.x[:, 0:H]).then_inc(s.loaded, 16)
+    g.sync.dma_start(T.y[:, H:H + W], T.x[:, :]).then_inc(s.stored, 16)
+
+    rr, rp = topo.addr(right, core)
+    lr, lp = topo.addr(left, core)
+    g.wait_ge(s.loaded, 32)
+    g.remote_dma_fused(
+        [
+            RemoteDMATransfer(dst_ids=[DstId(rid=rr, pnc=rp)], dma_engine_mask=0x1, remote_sem=s.arr_l,
+                              src=T.send[0], dst=T.land[0]),
+            RemoteDMATransfer(dst_ids=[DstId(rid=lr, pnc=lp)], dma_engine_mask=0x2, remote_sem=s.arr_r,
+                              src=T.send[1], dst=T.land[1]),
+        ],
+        local_sem=s.sent,
+    )
+
+    g.sync.wait_ge(s.arr_l, 1)
+    g.sync.dma_start(T.y[:, 0:H], T.land[0]).then_inc(s.stored, 16)
+    g.scalar.wait_ge(s.arr_r, 1)
+    g.scalar.dma_start(T.y[:, H + W:H + W + H], T.land[1]).then_inc(s.stored, 16)
+
+    g.wait_ge(s.sent, 2)
+    g.wait_ge(s.stored, 48)

@@ -1,12 +1,10 @@
-from concourse.bass import DstId, RemoteDMATransfer
-
 H = 2
 
 SCRATCH = {
     "send": ("dram", [2, 128, H], "bfloat16"),
     "land": ("dram", [2, 128, H], "bfloat16"),
 }
-SEMAPHORES = ["loaded", "sent", "arr_l", "arr_r", "stored"]
+SEMAPHORES = ["ld_far", "ld_near", "sent", "arr0", "arr1", "stored"]
 
 
 def rank_program(g, core, T, topo):
@@ -14,31 +12,26 @@ def rank_program(g, core, T, topo):
     if rank is None:
         return
     n = len(T.cores)
-    right = T.cores[(rank + 1) % n]
-    left = T.cores[(rank - 1) % n]
     W = T.x.shape[1]
     s = T.sem
+    peer = [T.cores[(rank + 1) % n], T.cores[(rank - 1) % n]]
+    edge = [T.x[:, W - H:W], T.x[:, 0:H]]
+    arr = [s.arr0, s.arr1]
+    far = 1 if topo.mates(core, peer[0]) else 0
+    near = 1 - far
 
-    g.sync.dma_start(T.send[0], T.x[:, W - H:W]).then_inc(s.loaded, 16)
-    g.scalar.dma_start(T.send[1], T.x[:, 0:H]).then_inc(s.loaded, 16)
+    g.sync.dma_start(T.send[far], edge[far]).then_inc(s.ld_far, 16)
+    g.sync.dma_start(T.send[near], edge[near]).then_inc(s.ld_near, 16)
     g.sync.dma_start(T.y[:, H:H + W], T.x[:, :]).then_inc(s.stored, 16)
 
-    rr, rp = topo.addr(right, core)
-    lr, lp = topo.addr(left, core)
-    g.wait_ge(s.loaded, 32)
-    g.remote_dma_fused(
-        [
-            RemoteDMATransfer(dst_ids=[DstId(rid=rr, pnc=rp)], dma_engine_mask=0x1, remote_sem=s.arr_l,
-                              src=T.send[0], dst=T.land[0]),
-            RemoteDMATransfer(dst_ids=[DstId(rid=lr, pnc=lp)], dma_engine_mask=0x2, remote_sem=s.arr_r,
-                              src=T.send[1], dst=T.land[1]),
-        ],
-        local_sem=s.sent,
-    )
+    for k, ld, eng in ((far, s.ld_far, 0x1), (near, s.ld_near, 0x2)):
+        rid, pid = topo.addr(peer[k], core)
+        g.wait_ge(ld, 16)
+        g.remote_dma(T.land[k], T.send[k], arr[k], s.sent, pid, rid, eng)
 
-    g.sync.wait_ge(s.arr_l, 1)
+    g.sync.wait_ge(s.arr0, 1)
     g.sync.dma_start(T.y[:, 0:H], T.land[0]).then_inc(s.stored, 16)
-    g.scalar.wait_ge(s.arr_r, 1)
+    g.scalar.wait_ge(s.arr1, 1)
     g.scalar.dma_start(T.y[:, H + W:H + W + H], T.land[1]).then_inc(s.stored, 16)
 
     g.wait_ge(s.sent, 2)

H = 2

SCRATCH = {
    "send": ("dram", [2, 128, H], "bfloat16"),
    "land": ("dram", [2, 128, H], "bfloat16"),
}
SEMAPHORES = ["ld_far", "ld_near", "sent", "arr0", "arr1", "stored"]


def rank_program(g, core, T, topo):
    rank = T.rank_of(core)
    if rank is None:
        return
    n = len(T.cores)
    W = T.x.shape[1]
    s = T.sem
    peer = [T.cores[(rank + 1) % n], T.cores[(rank - 1) % n]]
    edge = [T.x[:, W - H:W], T.x[:, 0:H]]
    arr = [s.arr0, s.arr1]
    far = 1 if topo.mates(core, peer[0]) else 0
    near = 1 - far

    g.sync.dma_start(T.send[far], edge[far]).then_inc(s.ld_far, 16)
    g.sync.dma_start(T.send[near], edge[near]).then_inc(s.ld_near, 16)
    g.sync.dma_start(T.y[:, H:H + W], T.x[:, :]).then_inc(s.stored, 16)

    for k, ld, eng in ((far, s.ld_far, 0x1), (near, s.ld_near, 0x2)):
        rid, pid = topo.addr(peer[k], core)
        g.wait_ge(ld, 16)
        g.remote_dma(T.land[k], T.send[k], arr[k], s.sent, pid, rid, eng)

    g.sync.wait_ge(s.arr0, 1)
    g.sync.dma_start(T.y[:, 0:H], T.land[0]).then_inc(s.stored, 16)
    g.scalar.wait_ge(s.arr1, 1)
    g.scalar.dma_start(T.y[:, H + W:H + W + H], T.land[1]).then_inc(s.stored, 16)

    g.wait_ge(s.sent, 2)
    g.wait_ge(s.stored, 48)
